import numpy as np
import ml_dtypes


def mxq(x, axis, fmt="e4m3"):
    dtype, down = {"e4m3": (ml_dtypes.float8_e4m3fn, 7), "e5m2": (ml_dtypes.float8_e5m2, 14)}[fmt]
    v = np.moveaxis(np.asarray(x, np.float32).astype(ml_dtypes.bfloat16).astype(np.float64), axis, -1)
    blocks = v.reshape(v.shape[:-1] + (-1, 32))
    amax = np.abs(blocks).max(-1, keepdims=True)
    byte = np.maximum(np.where(amax > 0, np.frexp(amax)[1] - 1 + 127, 0) - down, 1)
    scale = np.exp2(byte - 127.0)
    codes = (blocks / scale).astype(np.float32).astype(dtype).astype(np.float64)
    return np.moveaxis((codes * scale).reshape(v.shape), -1, axis)


WIDE = False


def mx_kscale(k):
    if not WIDE:
        return np.ones(k)
    levels = np.array([10, -10, 5, -5, 0])
    if k % 512:
        return np.exp2(np.random.permutation(np.resize(levels, k // 32))).repeat(32)
    a = np.empty((k // 512, 16))
    for p in range(k // 512):
        a[p, :8] = np.random.permutation(np.resize(levels, 8))
        for g in range(8):
            far = levels[np.abs(levels - a[p, g]) >= 10]
            a[p, g + 8] = far[np.random.randint(len(far))]
    return np.exp2(a.ravel()).repeat(32)


def f64(x):
    return np.asarray(x).astype(np.float64)


def striped(idx):
    return np.tile(idx.reshape(-1, 16).T, (8, 1)).astype(np.uint16)


def unstriped(offs):
    return offs[:16].T.reshape(-1).astype(np.int64)


E2M1 = np.array([0.0, 0.5, 1.0, 1.5, 2.0, 3.0, 4.0, 6.0, -0.0, -0.5, -1.0, -1.5, -2.0, -3.0, -4.0, -6.0])


def pack_weight(w, fmt):
    k, n = w.shape
    w = f64(np.asarray(w, np.float32).astype(ml_dtypes.bfloat16)).reshape(k // 32, 32, n)
    amax = np.abs(w).max(1)
    if fmt == "e4m3":
        byte = np.frexp(amax)[1] - 1 + 127 - 7
    else:
        mant, ex = np.frexp(amax / 6.0)
        byte = np.where(mant > 0.5, ex, ex - 1) + 127
    byte = np.clip(np.where(amax > 0, byte, 1), 1, 254)
    scaled = (w * np.exp2(127.0 - byte)[:, None, :]).reshape(k, n).astype(np.float32)
    by_word = np.ascontiguousarray(scaled.reshape(k // 512, 128, 4, n).transpose(0, 1, 3, 2))
    if fmt == "e4m3":
        words = by_word.astype(ml_dtypes.float8_e4m3fn).view(np.uint8)
    else:
        c = by_word.astype(ml_dtypes.float4_e2m1fn).view(np.uint8) & 0xF
        words = (c[..., 0::2] | (c[..., 1::2] << 4)).reshape(k // 512, 128, 2 * n)
    return np.ascontiguousarray(words), np.ascontiguousarray(byte.astype(np.uint8).reshape(k // 512, 16, n))


def unpack_weight(words, scales, fmt):
    g, _, n = scales.shape
    words = np.ascontiguousarray(words).reshape(g, 128, n, -1)
    if fmt == "e4m3":
        vals = words.view(ml_dtypes.float8_e4m3fn).astype(np.float64)
    else:
        nib = np.empty((g, 128, n, 4), np.uint8)
        nib[..., 0::2] = words & 0xF
        nib[..., 1::2] = words >> 4
        vals = E2M1[nib]
    vals = vals * np.repeat(np.exp2(scales.astype(np.float64) - 127.0), 8, axis=1)[..., None]
    return vals.transpose(0, 1, 3, 2).reshape(g * 512, n)


def gelu(v):
    return 0.5 * v * (1.0 + np.tanh(np.sqrt(2.0 / np.pi) * (v + 0.044715 * v**3)))


K, KA, KB, H, T, S, T2, T3, S2, P = 1536, 1024, 512, 1024, 2048, 1024, 2048, 2048, 512, 512

def setup_inputs():
    n = np.random.standard_normal
    s = mx_kscale(K)[:, None]
    u = mx_kscale(H)[:, None]
    tab_words, tab_scales = pack_weight(n((K, T)) * s, "e4m3")
    tab2_words, tab2_scales = pack_weight(n((H, T3)) / u / np.sqrt(H), "e4m3")
    w4_words, w4_scales = pack_weight(0.4 * n((KA, H)) / s[:KA] / np.sqrt(K), "e2m1")
    return {
        "tab_words": tab_words, "tab_scales": tab_scales,
        "tab2_words": tab2_words, "tab2_scales": tab2_scales,
        "w4_words": w4_words, "w4_scales": w4_scales,
        "w1": (0.4 * n((KB, H)) / s[KA:] / np.sqrt(K)).astype(np.float32),
        "b": np.random.uniform(-0.9, 0.9, H).astype(np.float32),
        "gain": (4.0 * np.exp(0.3 * n(H)) * u[:, 0]).astype(np.float32),
        "wgs": np.exp(0.3 * n((128, S))).astype(np.float32),
        "page0": (n((H, T2)) * u).astype(np.float32),
        "need": ((n((H, P)) + 0.5) * u).astype(np.float32),
        "price": (0.5 * n((S2, P))).astype(np.float32),
        "rate": np.exp(0.3 * n(S2)).astype(np.float32),
        "offs": striped(np.random.permutation(T)[:S]),
        "offs2": striped(np.random.permutation(T3)[:S2]),
        "offs3": striped(np.random.permutation(T2)[:S]),
        "offs4": striped(np.random.permutation(T2)[:P]),
    }

def reference(tab_words, tab_scales, tab2_words, tab2_scales, w4_words, w4_scales, w1, b, gain, wgs, page0, need, price, rate, offs, offs2, offs3, offs4):
    v = unpack_weight(tab_words, tab_scales, "e4m3")[:, unstriped(offs)]
    v2 = unpack_weight(tab2_words, tab2_scales, "e4m3")[:, unstriped(offs2)]
    w4 = unpack_weight(w4_words, w4_scales, "e2m1")
    y = w4.T @ v[:KA] + mxq(f64(w1), 0, "e4m3").T @ v[KA:]
    h = f64(gain)[:, None] * (y * np.cos(y + f64(b)[:, None]))
    page = f64(page0).copy()
    page[:, unstriped(offs3)] = np.tile(f64(wgs), (H // 128, 1)) * h
    x = np.minimum(page[:, unstriped(offs4)], f64(need))
    e = v2.T @ mxq(x, 0, "e4m3")
    return (e + f64(price)) * f64(rate)[:, None]

import math
from contextlib import ExitStack

import concourse.mybir as mybir
from concourse.masks import make_identity

K, KA, KB, H, T, S, T2, T3, S2, NP = 1536, 1024, 512, 1024, 2048, 1024, 2048, 2048, 512, 512
FLOPS = 2 * K * H * S + 2 * H * S2 * NP

F32 = mybir.dt.float32
BF16 = mybir.dt.bfloat16
I32 = mybir.dt.int32
U32 = mybir.dt.uint32
U16 = mybir.dt.uint16
U8 = mybir.dt.uint8
FP8X4 = mybir.dt.float8_e4m3fn_x4
FP4X4 = mybir.dt.float4_e2m1fn_x4
ALU = mybir.AluOpType
ACT = mybir.ActivationFunctionType

P = 128
PACK = 4
HALF = P * PACK
LANES = 16
ROUNDER = 1.5 * 2.0**23
TWO_PI = 2.0 * math.pi

LIST_CUTS = ((0, 256), (256, 256), (512, 512))
STEPS = ((0, 0, 256), (0, 256, 256), (0, 512, 512), (1, 0, 512), (1, 512, 512))


def tile_list_basket_substitute_scores_kernel(
    tc, tab_words, tab_scales, tab2_words, tab2_scales, w4_words, w4_scales,
    w1, b, gain, wgs, page0, need, price, rate, offs, offs2, offs3, offs4, out,
):
    nc = tc.nc
    with ExitStack() as ctx:
        keep = ctx.enter_context(tc.tile_pool(name="keep", bufs=1))
        work = ctx.enter_context(tc.tile_pool(name="work", bufs=2))
        psum = ctx.enter_context(tc.psum_pool(name="psum", bufs=1))
        banks = [[psum.tile([P, HALF], F32, name="bank%d_%d" % (g, i)) for i in range(2)] for g in range(2)]

        def columns(lst, j0, n):
            return lst[:, j0 // LANES : (j0 + n) // LANES]

        def load_list(src, name):
            t = keep.tile(list(src.shape), U16, name=name)
            nc.sync.dma_start(t[:], src)
            return t

        def load_words(src, name, tag, bufs, parts=1):
            t = work.tile([P, T], I32, name=name, tag=tag, bufs=bufs, align_bytes=64)
            for c0 in range(0, T, T // parts):
                cols = slice(c0, c0 + T // parts)
                nc.sync.dma_start(t[:, cols], src.rearrange("p t i -> p (t i)").bitcast(I32)[:, cols])
            return t

        def zeroed_plane(shape, name, engine):
            t = keep.tile(shape, U8, name=name, align_bytes=64)
            engine.memset(t[:].bitcast(I32), 0)
            return t

        def load_plane(plane, src):
            rows = 4 * src.shape[0]
            for q in range(4):
                nc.sync.dma_start(
                    plane[32 * q : 32 * q + rows, :].bitcast(I32),
                    src[:, 4 * q : 4 * q + 4, :].bitcast(I32),
                )

        def load_w1(r0, width, tag):
            t = keep.tile([P, PACK, width], F32, name="w1_raw%d" % r0, tag=tag, align_bytes=64)
            nc.sync.dma_start(t[:], w1[:, r0 : r0 + width].rearrange("(p i) r -> p i r", i=PACK))
            return t

        def load_w4(half):
            t = keep.tile([P, 2, 2 * HALF], U8, name="w4_codes%d" % half, align_bytes=64)
            nc.sync.dma_start(
                t[:].bitcast(I32),
                w4_words[:, :, 2 * half * HALF : 2 * (half + 1) * HALF].rearrange("a p n -> p a n").bitcast(I32),
            )
            return t

        def load_page(half, t):
            pg = work.tile([P, T2], F32, name="page%d_%d" % (half, t), tag="page", bufs=8, align_bytes=64)
            rows = page0[half * HALF : (half + 1) * HALF, :].rearrange("(p t) s -> p t s", t=PACK)
            nc.sync.dma_start(pg[:], rows[:, t, :])
            return pg

        def load_wgs(j0, j1):
            src = wgs.rearrange("(q t) j -> q t j", t=PACK)
            for g in range(4):
                nc.sync.dma_start(wgs_sb[32 * g : 32 * g + 32, :, j0:j1], src[:, :, j0:j1])

        def load_need(half):
            t = work.tile([P, PACK, NP], F32, name="need%d" % half, tag="words", bufs=3, align_bytes=64)
            nc.sync.dma_start(t[:], need[half * HALF : (half + 1) * HALF, :].rearrange("(p t) j -> p t j", t=PACK))
            return t

        v_planes = keep.tile([P, 2, T], U8, align_bytes=64)
        nc.vector.memset(v_planes[:, 0, :].bitcast(I32), 0)
        nc.gpsimd.memset(v_planes[:, 1, :].bitcast(I32), 0)
        w4_plane = zeroed_plane([P, 2, H], "w4_plane", nc.vector)
        plane_v2 = zeroed_plane([P, T3], "plane_v2", nc.gpsimd)
        wgs_sb = keep.tile([P, PACK, S], F32)

        def load_side_by_side(plane, src):
            for q in range(4):
                nc.sync.dma_start(
                    plane[32 * q : 32 * q + 4, :, :].bitcast(I32),
                    src[:, 4 * q : 4 * q + 4, :].rearrange("a q n -> q a n").bitcast(I32),
                )

        idx = load_list(offs, "idx")
        words = [load_words(tab_words[0], "tab_words0", "words", 3, 2)]
        b_sb = keep.tile([P, 2, PACK], F32)
        gain_sb = keep.tile([P, 2, PACK], F32)
        nc.sync.dma_start(b_sb[:], b.rearrange("(h p t) -> p h t", h=2, t=PACK))
        nc.sync.dma_start(gain_sb[:], gain.rearrange("(h p t) -> p h t", h=2, t=PACK))
        idx3 = load_list(offs3, "idx3")
        w1_raw = [[load_w1(0, HALF // 2, "late_codes"), load_w1(HALF // 2, HALF // 2, "late_planes")]]
        load_side_by_side(v_planes, tab_scales[0:2])
        words.append(load_words(tab_words[1], "tab_words1", "words", 3))
        for q in range(4):
            nc.sync.dma_start(
                v_planes[32 * q + 4 : 32 * q + 8, 0, :].bitcast(I32), tab_scales[2, 4 * q : 4 * q + 4, :].bitcast(I32)
            )
        words.append(load_words(tab_words[2], "tab_words2", "words", 3))
        load_side_by_side(w4_plane, w4_scales)
        w4_codes = [load_w4(0)]
        idx2 = load_list(offs2, "idx2")
        load_plane(plane_v2, tab2_scales)
        words2 = [load_words(tab2_words[0], "tab2_words0", "words2", 2)]
        load_wgs(0, 256)
        words2.append(load_words(tab2_words[1], "tab2_words1", "words2", 2))
        pages = {(0, t): load_page(0, t) for t in range(PACK)}
        load_wgs(256, 512)
        w1_raw.append([load_w1(HALF, HALF, "w1_raw_second")])
        load_wgs(512, S)
        w4_codes.append(load_w4(1))
        idx4 = load_list(offs4, "idx4")
        need_sb = [load_need(0)]
        for t in range(PACK):
            pages[(1, t)] = load_page(1, t)
        need_sb.append(load_need(1))
        price_sb = work.tile([P, S2 // P, NP], F32, tag="words", bufs=3, align_bytes=64)
        nc.sync.dma_start(price_sb[:], price.rearrange("(c p) j -> p c j", p=P))

        rate_sb = keep.tile([P, S2 // P], F32)
        with nc.allow_non_contiguous_dma(reason="one value a candidate, candidates on partitions"):
            nc.sync.dma_start(rate_sb[:], rate.rearrange("(c p) -> p c", p=P))
        ident = keep.tile([P, P], F32)
        make_identity(nc, ident[:])

        b_flat = b_sb[:].rearrange("p h t -> p (h t)")
        m_int = keep.tile([P, 2 * PACK], I32)
        nc.vector.tensor_scalar(m_int[:], b_flat, 1.0 / math.pi, ROUNDER, ALU.mult, ALU.add)
        m_pi = keep.tile([P, 2 * PACK], F32)
        nc.vector.tensor_scalar(m_pi[:], m_int[:], -ROUNDER, -math.pi, ALU.add, ALU.mult)
        m_odd = keep.tile([P, 2 * PACK], I32)
        nc.vector.tensor_scalar(m_odd[:], m_int[:], 1, None, ALU.bitwise_and)
        phase = keep.tile([P, 2 * PACK], F32)
        nc.vector.tensor_tensor(phase[:], b_flat, m_pi[:], ALU.add)
        signed = keep.tile([P, 2 * PACK], F32)
        nc.vector.tensor_scalar(signed[:], m_odd[:], -2.0 * TWO_PI, TWO_PI, ALU.mult, ALU.add)
        amp = keep.tile([P, 2 * PACK], F32)
        nc.vector.tensor_tensor(amp[:], signed[:], gain_sb[:].rearrange("p h t -> p (h t)"), ALU.mult)

        def quantise_w1(half, room):
            width = HALF * PACK // len(w1_raw[half])
            for part, raw in enumerate(w1_raw[half]):
                nc.scalar.copy(
                    room[:, part * width : (part + 1) * width].rearrange("p (r i) -> p r i", i=PACK),
                    raw[:].rearrange("p i r -> p r i"),
                )
            codes = keep.tile([P, HALF], U32, name="w1_codes%d" % half, align_bytes=64)
            plane = keep.tile([P, HALF], U8, name="w1_plane%d" % half, align_bytes=64)
            nc.vector.quantize_mx(
                out=codes[:].bitcast(FP8X4), scales=plane[:], in_=room
            )
            return codes, plane

        def gather(dst, window, lst, j0, n):
            nc.vector.tensor_copy(dst, window.indirect(columns(lst, j0, n)))

        windows = [w[:].bitcast(U32) for w in words]
        v_codes0 = keep.tile([P, S], U32, align_bytes=64)
        gather(v_codes0[:], windows[0], idx, 0, S)
        early_planes = keep.tile([P, 2, S // 2], U8, align_bytes=64)
        for g in (1, 0):
            gather(early_planes[:, g, :], v_planes[:, g, :], idx, 0, S // 2)
        early_codes = keep.tile([P, 2, S // 2], U32, align_bytes=64)
        gather(early_codes[:, 0, :], windows[1], idx, 0, S // 2)
        w1_grouped = work.tile([P, HALF * PACK], BF16, tag="slots", bufs=1, align_bytes=64)
        w1_q = [quantise_w1(0, w1_grouped[:])]
        for j0 in (0, S // 4):
            gather(early_codes[:, 1, j0 : j0 + S // 4], windows[2], idx, j0, S // 4)
        late_planes = keep.tile([P, 3, S // 2], U8, tag="late_planes", align_bytes=64)
        late_codes = keep.tile([P, 4, S // 2], U32, tag="late_codes", align_bytes=64)
        for g in range(2):
            gather(late_planes[:, g, :], v_planes[:, g, :], idx, S // 2, S // 2)
            gather(late_codes[:, g, :], windows[1 + g], idx, S // 2, S // 2)
        gather(late_planes[:, 2, :], plane_v2[:], idx2, 0, S2)
        for a in range(2):
            gather(late_codes[:, 2 + a, :], words2[a][:].bitcast(U32), idx2, 0, S2)

        def picked(a, j):
            planes, codes = (early_planes, early_codes) if j < S // 2 else (late_planes, late_codes)
            cols = slice(j % (S // 2), j % (S // 2) + P)
            if a == 0:
                return v_codes0[:, j : j + P], planes[:, 0, cols]
            return codes[:, a - 1, cols], (planes[:, 1, cols] if a == 1 else planes[4:P, 0, cols])

        def first_product(half, j0, n, y_banks):
            tiles = n // P
            turns = work.tile([P, PACK, tiles, P], F32, name="turns", align_bytes=64)
            rows = slice(half * HALF, (half + 1) * HALF)
            for jt in range(tiles):
                y_t = y_banks[jt % 2]
                moving = [
                    (w4_codes[half][:, 0, :].bitcast(FP4X4), w4_plane[:, 0, rows]),
                    (w4_codes[half][:, 1, :].bitcast(FP4X4), w4_plane[:, 1, rows]),
                    (w1_q[half][0][:].bitcast(FP8X4), w1_q[half][1][:]),
                ]
                for a in range(3):
                    codes, plane = picked(a, j0 + jt * P)
                    nc.tensor.matmul_mx(
                        out=y_t[:], lhsT=codes.bitcast(FP8X4), lhsT_scale=plane,
                        rhs=moving[a][0], rhs_scale=moving[a][1], start=(a == 0), stop=(a == 2),
                    )
                nc.scalar.activation(
                    turns[:, :, jt, :], y_t[:].rearrange("j (q t) -> j t q", t=PACK), ACT.Copy, scale=1.0 / TWO_PI
                )
            return turns

        def put_pair(half, j0, n, turns, t0):
            tiles = n // P
            folded = work.tile([P, 2, n], F32, name="folded", bufs=1)
            for i in range(2):
                t = t0 + i
                whole_int = work.tile([P, n], U32, name="whole_int")
                nc.scalar.activation(
                    whole_int[:], turns[:, t, :, :].rearrange("j c q -> j (c q)"), ACT.Copy, bias=ROUNDER
                )
                minus_whole = work.tile([P, n], F32, name="minus_whole", bufs=3)
                nc.scalar.activation(minus_whole[:], whole_int[:], ACT.Copy, scale=-1.0, bias=ROUNDER)
                frac = banks[t0 // 2][i]
                for jt in range(tiles):
                    cols = slice(jt * P, (jt + 1) * P)
                    nc.tensor.matmul(frac[:, cols], turns[:, t, jt, :], ident[:], start=True, stop=False, is_transpose=True)
                    nc.tensor.matmul(frac[:, cols], minus_whole[:, cols], ident[:], start=False, stop=True, is_transpose=True)
            for i in range(2):
                row = half * PACK + t0 + i
                nc.scalar.activation(
                    folded[:, i, :], banks[t0 // 2][i][:, :n], ACT.Abs, bias=phase[:, row : row + 1], scale=TWO_PI
                )
            u_banks = []
            for i in range(2):
                u_bank = psum.tile([P, HALF], F32, name="u_bank", tag="rows", bufs=4)
                for jt in range(tiles):
                    nc.tensor.transpose(u_bank[:, jt * P : (jt + 1) * P], turns[:, t0 + i, jt, :], ident[:])
                u_banks.append(u_bank)
            cosine = work.tile([P, 2, n], F32, name="cosine")
            nc.scalar.activation(cosine[:], folded[:], ACT.Sin, bias=math.pi / 2, scale=-1.0)
            h = work.tile([P, 2, n], F32, name="h")
            for i in range(2):
                row = half * PACK + t0 + i
                nc.vector.scalar_tensor_tensor(
                    h[:, i, :], u_banks[i][:, :n], amp[:, row : row + 1], cosine[:, i, :], ALU.mult, ALU.mult
                )
            for i in range(2):
                t = t0 + i
                nc.vector.tensor_tensor(
                    pages[(half, t)][:].indirect(columns(idx3, j0, n)), h[:, i, :], wgs_sb[:, t, j0 : j0 + n], ALU.mult
                )

        def quantise_x(half):
            slots = work.tile([P, PACK, NP], F32, name="slots", bufs=1, align_bytes=64)
            for t in range(PACK):
                nc.vector.tensor_copy(slots[:, t, :], pages[(half, t)][:].indirect(idx4[:]))
            codes = keep.tile([P, NP], U32, name="x_codes%d" % half, align_bytes=64)
            plane = keep.tile([P, NP], U8, name="x_plane%d" % half, align_bytes=64)
            width = NP // 2
            grouped = []
            for part in range(2):
                js = slice(part * width, (part + 1) * width)
                g = work.tile([P, width, PACK], BF16, name="x_grouped", align_bytes=64)
                nc.vector.tensor_tensor(
                    g[:].rearrange("p (c i) t -> p c t i", i=4),
                    slots[:, :, js].rearrange("p t (c i) -> p c t i", i=4),
                    need_sb[half][:, :, js].rearrange("p t (c i) -> p c t i", i=4),
                    ALU.min,
                )
                grouped.append(g)
            for part in range(2):
                js = slice(part * width, (part + 1) * width)
                nc.vector.quantize_mx(
                    out=codes[:, js].bitcast(FP8X4), scales=plane[:, js],
                    in_=grouped[part][:].rearrange("p j t -> p (j t)"),
                )
            return codes, plane

        x_q = []
        turns = first_product(*STEPS[0], banks[1])
        for s, (half, j0, n) in enumerate(STEPS):
            put_pair(half, j0, n, turns, 0)
            ahead = first_product(*STEPS[s + 1], banks[0]) if s + 1 < len(STEPS) else turns
            put_pair(half, j0, n, turns, 2)
            if s == 1:
                w1_q.append(quantise_w1(1, turns[:].rearrange("j t c q -> j (t c q)").bitcast(BF16)))
            turns = ahead
            if j0 + n == S:
                x_q.append(quantise_x(half))

        result = turns[:].rearrange("p t c q -> p t (c q)")
        for c in range(S2 // P):
            nc.scalar.activation(result[:, c, :], price_sb[:, c, :], ACT.Copy, scale=rate_sb[:, c : c + 1])
        scores = [psum.tile([P, NP], F32, name="score%d" % c, tag="rows", bufs=4) for c in range(S2 // P)]
        for a in range(2):
            for c in range(S2 // P):
                cols = slice(c * P, (c + 1) * P)
                nc.tensor.matmul_mx(
                    out=scores[c][:], lhsT=late_codes[:, 2 + a, cols].bitcast(FP8X4), lhsT_scale=late_planes[4 * a : P, 2, cols],
                    rhs=x_q[a][0][:].bitcast(FP8X4), rhs_scale=x_q[a][1][:], start=(a == 0), stop=(a == 1),
                )
        for c in range(S2 // P):
            nc.vector.scalar_tensor_tensor(
                result[:, c, :], scores[c][:], rate_sb[:, c : c + 1], result[:, c, :], ALU.mult, ALU.add
            )
            nc.sync.dma_start(out[c * P : (c + 1) * P, :], result[:, c, :])
